import numpy as np
import ml_dtypes


def mxq(x, axis, fmt="e4m3"):
    dtype, down = {"e4m3": (ml_dtypes.float8_e4m3fn, 7), "e5m2": (ml_dtypes.float8_e5m2, 14)}[fmt]
    v = np.moveaxis(np.asarray(x, np.float32).astype(ml_dtypes.bfloat16).astype(np.float64), axis, -1)
    blocks = v.reshape(v.shape[:-1] + (-1, 32))
    amax = np.abs(blocks).max(-1, keepdims=True)
    byte = np.maximum(np.where(amax > 0, np.frexp(amax)[1] - 1 + 127, 0) - down, 1)
    scale = np.exp2(byte - 127.0)
    codes = (blocks / scale).astype(np.float32).astype(dtype).astype(np.float64)
    return np.moveaxis((codes * scale).reshape(v.shape), -1, axis)


WIDE = False


def mx_kscale(k):
    if not WIDE:
        return np.ones(k)
    levels = np.array([10, -10, 5, -5, 0])
    if k % 512:
        return np.exp2(np.random.permutation(np.resize(levels, k // 32))).repeat(32)
    a = np.empty((k // 512, 16))
    for p in range(k // 512):
        a[p, :8] = np.random.permutation(np.resize(levels, 8))
        for g in range(8):
            far = levels[np.abs(levels - a[p, g]) >= 10]
            a[p, g + 8] = far[np.random.randint(len(far))]
    return np.exp2(a.ravel()).repeat(32)


BF16 = ml_dtypes.bfloat16


def bf(x):
    return np.asarray(x, np.float32).astype(BF16)


def f64(x):
    return np.asarray(x).astype(np.float64)

def planes(Y):
    n, m = Y.shape
    b = f64(bf(Y)).reshape(n // 32, 32, m)
    amax = np.abs(b).max(1)
    byte = np.clip(np.where(amax > 0, np.frexp(amax)[1] - 1 + 127 - 7, 1), 1, 254)
    codes = (b * np.exp2(127.0 - byte)[:, None, :]).reshape(n, m).astype(np.float32).astype(ml_dtypes.float8_e4m3fn).view(np.uint8)
    words = codes.reshape(n // 512, 128, 4, m).transpose(0, 1, 3, 2)
    return np.ascontiguousarray(words), np.ascontiguousarray(byte.astype(np.uint8).reshape(n // 512, 16, m))


T, J, M = 1024, 1024, 1024


def sinh_exp(a):
    return (np.exp(a) - np.exp(-a)) / 2.0


def setup_inputs():
    s, u = mx_kscale(J), mx_kscale(T)
    return {
        "y0": bf(np.random.standard_normal((T, J)) * 32.0 / np.sqrt(J) / s),
        "y1": bf(np.random.standard_normal((T, M))),
        "z": bf(np.random.standard_normal((T, J)) / u[:, None]),
        "theta": bf(np.random.standard_normal((J, M)) * 0.5),
        "v": bf((1.0 + 0.1 * np.random.standard_normal(J)) * s),
        "lam": bf((1.0 + 0.1 * np.random.standard_normal(T)) * u),
        "mu": bf(np.random.standard_normal(M) * 0.5),
    }


def core(y0, y1, z, theta, v, lam, mu):
    th = f64(theta)
    n_time = z.shape[0]
    w = 0.05 * f64(v)[:, None] * sinh_exp(th)
    fit = mxq(f64(y0), 1, "e4m3") @ mxq(w, 0, "e4m3")
    r = fit + f64(mu)[None, :] - f64(y1)
    rl = f64(lam)[:, None] * r
    g = (mxq(f64(z), 0, "e4m3").T @ mxq(rl, 0, "e4m3")) / np.sqrt(n_time)
    theta2 = th - 0.3 * g
    return sinh_exp(theta2)


def reference(y0, y1, z, theta, v, lam, mu):
    R_out = core(y0, y1, z, theta, v, lam, mu)
    words, scales = planes(R_out)
    return R_out, words, scales

@@ -1,0 +1,417 @@
+import math
+from contextlib import ExitStack
+
+import concourse.mybir as mybir
+from concourse.masks import make_identity
+
+F32 = mybir.dt.float32
+BF16 = mybir.dt.bfloat16
+U32 = mybir.dt.uint32
+I32 = mybir.dt.int32
+U8 = mybir.dt.uint8
+FP8X4 = mybir.dt.float8_e4m3fn_x4
+ALU = mybir.AluOpType
+ACT = mybir.ActivationFunctionType
+
+N = 1024
+FLOPS = 2 * 2 * N * N * N
+P = 128
+PACK = 4
+PASS = P * PACK
+PASSES = N // PASS
+BLOCKS = N // P
+CHUNK = 256
+CHUNKS = N // CHUNK
+W_FACTOR = 0.05 / 2
+STEP = -0.3 / math.sqrt(N)
+LN_HALF = math.log(0.5)
+LN_FLOOR = 2.0 ** -64
+LAG = 4
+ROUND_ON_VECTOR_FROM = 12
+RL_BUFS = 3
+UNITS = BLOCKS * PASSES
+W_AHEAD = 7
+Y0_ON_VECTOR = 2
+EARLY_BLOCKS = 5
+W_STRIDE = 2
+
+
+def tile_instrumentedsyntheticcontrolhypentropyst_x1_kernel(
+    tc, y0, y1, z, theta, v, lam, mu, out_0, out_1, out_2
+):
+    nc = tc.nc
+    with ExitStack() as ctx:
+        keep = ctx.enter_context(tc.tile_pool(name="keep", bufs=1))
+        work = ctx.enter_context(tc.tile_pool(name="work", bufs=2))
+        psum = ctx.enter_context(tc.psum_pool(name="psum", bufs=1))
+        ctx.enter_context(tc.manual_schedule())
+
+        def kept(name, shape, dtype):
+            return keep.tile(shape, dtype, name=name, align_bytes=64)
+
+        def passing(name, shape, dtype, bufs=2):
+            return work.tile(shape, dtype, name=name, align_bytes=64, bufs=bufs)
+
+        def bank(tag, shape, dtype):
+            return psum.tile(shape, dtype, name=tag)
+
+        def slot_rows(x, g):
+            return x[g * PASS : (g + 1) * PASS, :].rearrange("(p t) c -> p t c", t=PACK)
+
+        v_sb = kept("v_sb", [P, PASSES, PACK], BF16)
+        lam_sb = kept("lam_sb", [P, PASSES, PACK], BF16)
+        mu_rows = kept("mu_rows", [P, P], BF16)
+        y0_sb = [[kept("y0_%d_%d" % (g, t), [P, N], BF16) for t in range(PACK)] for g in range(PASSES)]
+        theta_sb = [[kept("theta_%d_%d" % (c, g), [P, PACK, CHUNK], BF16) for g in range(PASSES)] for c in range(CHUNKS)]
+        y1_sb = [[kept("y1_%d_%d" % (c, g), [P, PACK, CHUNK], BF16) for g in range(PASSES)] for c in range(CHUNKS)]
+        z_sb = [[kept("z_%d_%d" % (h, g), [P, PACK, PASS], BF16) for g in range(PASSES)] for h in range(PASSES)]
+        ident_f32 = kept("ident_f32", [P, P], F32)
+        ident_bf16 = kept("ident_bf16", [P, P], BF16)
+
+        def load_columns(tiles, x, c):
+            for g in range(PASSES):
+                width = tiles[c][g].shape[2]
+                nc.sync.dma_start(out=tiles[c][g][:], in_=slot_rows(x, g)[:, :, c * width : (c + 1) * width])
+
+        def load_y0(g):
+            for t in range(PACK):
+                nc.sync.dma_start(out=y0_sb[g][t][:], in_=slot_rows(y0, g)[:, t, :])
+
+        make_identity(nc, ident_f32[:])
+        nc.gpsimd.memset(mu_rows[:], 0.0)
+        make_identity(nc, ident_bf16[:])
+
+        def load_piece(tiles, x, c, g):
+            width = tiles[c][g].shape[2]
+            nc.sync.dma_start(out=tiles[c][g][:], in_=slot_rows(x, g)[:, :, c * width : (c + 1) * width])
+
+        nc.sync.dma_start(out=v_sb[:], in_=v.rearrange("(g p t) -> p g t", g=PASSES, t=PACK))
+        for g in range(PASSES):
+            load_piece(z_sb, z, 0, g)
+            load_piece(theta_sb, theta, 0, g)
+        load_y0(0)
+        nc.sync.dma_start(out=mu_rows[0:BLOCKS, :], in_=mu.rearrange("(b m) -> b m", m=P))
+        load_piece(theta_sb, theta, 1, 0)
+        load_piece(z_sb, z, 1, 0)
+        load_y0(1)
+        load_piece(y1_sb, y1, 0, 0)
+        nc.sync.dma_start(out=lam_sb[:], in_=lam.rearrange("(g p t) -> p g t", g=PASSES, t=PACK))
+        load_piece(theta_sb, theta, 1, 1)
+        load_piece(z_sb, z, 1, 1)
+        load_piece(y1_sb, y1, 0, 1)
+        load_columns(y1_sb, y1, 1)
+        for c in range(2, CHUNKS):
+            load_columns(theta_sb, theta, c)
+            load_columns(y1_sb, y1, c)
+
+        slots = PASSES * PACK
+        v_flat = v_sb[:].rearrange("p g t -> p (g t)")
+        v_abs = kept("v_abs", [P, slots], F32)
+        v_pos = kept("v_pos", [P, slots], F32)
+        v_neg = kept("v_neg", [P, slots], F32)
+        v_sign = kept("v_sign", [P, slots], F32)
+        v_sign_neg = kept("v_sign_neg", [P, slots], F32)
+        v_log = kept("v_log", [P, slots], F32)
+        nc.vector.scalar_tensor_tensor(out=v_abs[:], in0=v_flat, scalar=-1.0, in1=v_flat, op0=ALU.mult, op1=ALU.max)
+        nc.vector.tensor_scalar(out=v_pos[:], in0=v_flat, scalar1=0.0, scalar2=None, op0=ALU.is_gt)
+        nc.vector.tensor_scalar(out=v_neg[:], in0=v_flat, scalar1=0.0, scalar2=None, op0=ALU.is_lt)
+        nc.scalar.activation(out=v_log[:], in_=v_abs[:], func=ACT.Ln, scale=W_FACTOR, bias=LN_FLOOR)
+        nc.vector.tensor_tensor(out=v_sign[:], in0=v_pos[:], in1=v_neg[:], op=ALU.subtract)
+        nc.vector.tensor_tensor(out=v_sign_neg[:], in0=v_neg[:], in1=v_pos[:], op=ALU.subtract)
+
+        y0_words = [kept("y0_words%d" % g, [P, PASSES, PASS, 2], F32) for g in range(PASSES)]
+        y0_codes = [kept("y0_codes%d" % g, [P, N], U32) for g in range(PASSES)]
+        y0_scales = [kept("y0_scales%d" % g, [P, N], U8) for g in range(PASSES)]
+        y0_banks = ["turn0", "turn1", "grad0", "grad1"]
+
+        def y0_slot(g, t, copy):
+            turned = bank(y0_banks[t], [P, PASSES, 2, P], F32)
+            words = y0_sb[g][t][:].bitcast(F32)
+            for k in range(PASSES):
+                for u in range(2):
+                    nc.tensor.transpose(turned[:, k, u, :], words[:, 2 * P * k + u : 2 * P * (k + 1) : 2], ident_f32[:])
+            copy(
+                out=y0_words[g][:, :, t * P : (t + 1) * P, :], in_=turned[:].rearrange("p k u r -> p k r u")
+            )
+
+        def y0_quant(g):
+            nc.vector.quantize_mx(
+                out=y0_codes[g][:].bitcast(FP8X4),
+                scales=y0_scales[g][:],
+                in_=y0_words[g][:].rearrange("p k c u -> p (k c u)").bitcast(BF16),
+            )
+
+        w_codes = [kept("w_codes%d" % c, [P, PASSES, CHUNK], U32) for c in range(CHUNKS)]
+        w_scales = [kept("w_scales%d" % c, [P, PASSES, CHUNK], U8) for c in range(CHUNKS)]
+        w_state = {}
+
+        def w_exp(c, g):
+            up = passing("w_up", [P, PACK, CHUNK], F32)
+            down = passing("w_down", [P, PACK, CHUNK], F32)
+            for t in range(PACK):
+                s = g * PACK + t
+                for dst, sign in ((up, v_sign), (down, v_sign_neg)):
+                    nc.scalar.activation(
+                        out=dst[:, t, :], in_=theta_sb[c][g][:, t, :], func=ACT.Exp,
+                        scale=sign[:, s : s + 1], bias=v_log[:, s : s + 1],
+                    )
+            w_state[c, g] = (up, down)
+
+        def w_sub(c, g):
+            up, down = w_state[c, g]
+            packed = passing("w_packed", [P, CHUNK, PACK], BF16)
+            nc.vector.tensor_tensor(
+                out=packed[:].rearrange("p (m i) t -> p m t i", i=2),
+                in0=up[:].rearrange("p t (m i) -> p m t i", i=2),
+                in1=down[:].rearrange("p t (m i) -> p m t i", i=2),
+                op=ALU.subtract,
+            )
+            w_state[c, g] = packed
+
+        def w_quant(c, g):
+            nc.vector.quantize_mx(
+                out=w_codes[c][:, g, :].bitcast(FP8X4),
+                scales=w_scales[c][:, g, :],
+                in_=w_state[c, g][:].rearrange("p m t -> p (m t)"),
+            )
+
+        z_codes = [[kept("z_codes%d_%d" % (h, g), [P, PASS], U32) for g in range(PASSES)] for h in range(PASSES)]
+        z_scales = [[kept("z_scales%d_%d" % (h, g), [P, PASS], U8) for g in range(PASSES)] for h in range(PASSES)]
+        z_state = {}
+
+        def z_pack(h, g):
+            packed = passing("z_packed", [P, PACK, P, PACK], BF16)
+            nc.vector.tensor_copy(
+                out=packed[:].rearrange("p s (q i) t -> p q s i t", i=2),
+                in_=z_sb[h][g][:].rearrange("p t (q i s) -> p q s i t", i=2, s=PACK),
+            )
+            z_state[h, g] = packed
+
+        def z_quant(h, g):
+            nc.vector.quantize_mx(
+                out=z_codes[h][g][:].bitcast(FP8X4),
+                scales=z_scales[h][g][:],
+                in_=z_state[h, g][:].rearrange("p s q t -> p (s q t)"),
+            )
+
+        mu_col = kept("mu_col", [P, BLOCKS], F32)
+
+        def mu_turn():
+            turned = bank("y1_bank1", [P, P], BF16)
+            nc.tensor.transpose(turned[:], mu_rows[:], ident_bf16[:])
+            nc.scalar.copy(out=mu_col[:], in_=turned[:, 0:BLOCKS])
+
+        y1_t, fit, resid, back, rl, rl_q = {}, {}, {}, {}, {}, {}
+
+        def place(n):
+            b, g = divmod(n, PASSES)
+            c, half = divmod(b, CHUNK // P)
+            return b, g, c, slice(half * P, (half + 1) * P)
+
+        def y1_turn(n):
+            b, g, c, cols = place(n)
+            turned = bank("y1_bank%d" % g, [P, PACK, P], BF16)
+            for t in range(PACK):
+                nc.tensor.transpose(turned[:, t, :], y1_sb[c][g][:, t, cols], ident_bf16[:])
+            y1_t[n] = turned
+
+        def y1_copy(n):
+            dst = passing("y1_t", [P, PASS], BF16, bufs=3)
+            nc.scalar.copy(out=dst[:], in_=y1_t[n][:].rearrange("p t r -> p (t r)"))
+            y1_t[n] = dst
+
+        def fit_matmul(n):
+            b, g, c, cols = place(n)
+            acc = bank("fit%d" % g, [P, PASS], F32)
+            for k in range(PASSES):
+                nc.tensor.matmul_mx(
+                    out=acc[:],
+                    lhsT=w_codes[c][:, k, cols].bitcast(FP8X4),
+                    lhsT_scale=w_scales[c][:, k, cols],
+                    rhs=y0_codes[g][:, k * PASS : (k + 1) * PASS].bitcast(FP8X4),
+                    rhs_scale=y0_scales[g][:, k * PASS : (k + 1) * PASS],
+                    start=(k == 0),
+                    stop=(k == PASSES - 1),
+                )
+            fit[n] = acc
+
+        def residual(n):
+            b, g, c, cols = place(n)
+            r = passing("resid", [P, PASS], F32)
+            nc.vector.scalar_tensor_tensor(
+                out=r[:], in0=fit[n][:], scalar=mu_col[:, b : b + 1], in1=y1_t[n][:],
+                op0=ALU.add, op1=ALU.subtract,
+            )
+            resid[n] = r
+
+        def residual_turn(n):
+            turned = bank("turn%d" % (n % PASSES), [P, PACK, P], F32)
+            for t in range(PACK):
+                nc.tensor.transpose(turned[:, t, :], resid[n][:, t * P : (t + 1) * P], ident_f32[:])
+            back[n] = turned
+
+        def weigh(n):
+            b, g, c, cols = place(n)
+            if g == 0:
+                rl[b] = passing("rl_packed", [P, PASSES, P, PACK], BF16)
+            nc.vector.tensor_tensor(
+                out=rl[b][:, g, :, :],
+                in0=back[n][:].rearrange("p t m -> p m t"),
+                in1=lam_sb[:, g, :].unsqueeze(1).to_broadcast([P, P, PACK]),
+                op=ALU.mult,
+            )
+
+        def rl_quant(b):
+            codes = passing("rl_codes", [P, PASSES * P], U32, bufs=RL_BUFS)
+            scales = passing("rl_scales", [P, PASSES * P], U8, bufs=RL_BUFS)
+            nc.vector.quantize_mx(
+                out=codes[:].bitcast(FP8X4), scales=scales[:], in_=rl[b][:].rearrange("p g m t -> p (g m t)")
+            )
+            rl_q[b] = (codes, scales)
+
+        grad, stepped, exps, result, rounded, out_codes = {}, {}, {}, {}, {}, {}
+        out_scales = kept("out_scales", [P, PASSES, N], U8)
+
+        def grad_matmul(n):
+            b, h, c, cols = place(n)
+            codes, scales = rl_q[b]
+            acc = bank("grad%d" % h, [P, PACK, P], F32)
+            for s in range(PACK):
+                for g in range(PASSES):
+                    nc.tensor.matmul_mx(
+                        out=acc[:, s, :],
+                        lhsT=z_codes[h][g][:, s * P : (s + 1) * P].bitcast(FP8X4),
+                        lhsT_scale=z_scales[h][g][:, s * P : (s + 1) * P],
+                        rhs=codes[:, g * P : (g + 1) * P].bitcast(FP8X4),
+                        rhs_scale=scales[:, g * P : (g + 1) * P],
+                        start=(g == 0),
+                        stop=(g == PASSES - 1),
+                    )
+            grad[n] = acc
+
+        def dual_step(n):
+            b, h, c, cols = place(n)
+            stepped[n] = passing("theta2", [P, PACK, P], F32, bufs=3)
+            nc.vector.scalar_tensor_tensor(
+                out=stepped[n][:], in0=grad[n][:], scalar=STEP, in1=theta_sb[c][h][:, :, cols],
+                op0=ALU.mult, op1=ALU.add,
+            )
+
+        def out_exp(n):
+            up = passing("out_up", [P, PACK, P], F32, bufs=3)
+            down = passing("out_down", [P, PACK, P], F32, bufs=3)
+            nc.scalar.activation(out=up[:], in_=stepped[n][:], func=ACT.Exp, scale=1.0, bias=LN_HALF)
+            nc.scalar.activation(out=down[:], in_=stepped[n][:], func=ACT.Exp, scale=-1.0, bias=LN_HALF)
+            exps[n] = (up, down)
+
+        def out_sub(n):
+            b, h, c, cols = place(n)
+            up, down = exps[n]
+            res = passing("result", [P, PACK, P], F32, bufs=5)
+            nc.vector.tensor_tensor(out=res[:], in0=up[:], in1=down[:], op=ALU.subtract)
+            nc.sync.dma_start(out=slot_rows(out_0, h)[:, :, b * P : (b + 1) * P], in_=res[:])
+            result[n] = res
+
+        def out_round(n, copy):
+            packed = passing("out_packed", [P, P, PACK], BF16, bufs=3)
+            copy(
+                out=packed[:].rearrange("p (m i) s -> p m s i", i=2),
+                in_=result[n][:].rearrange("p s (m i) -> p m s i", i=2),
+            )
+            rounded[n] = packed
+
+        def out_quant(n):
+            b, h, c, cols = place(n)
+            if h == 0:
+                out_codes[b] = passing("out_codes", [P, PASSES, P], U32, bufs=3)
+            nc.vector.quantize_mx(
+                out=out_codes[b][:, h, :].bitcast(FP8X4),
+                scales=out_scales[:, h, b * P : (b + 1) * P],
+                in_=rounded[n][:].rearrange("p m s -> p (m s)"),
+            )
+            if h == PASSES - 1:
+                words = out_1.rearrange("h p m s -> p h (m s)").bitcast(I32)
+                nc.sync.dma_start(out=words[:, :, b * P : (b + 1) * P], in_=out_codes[b][:].bitcast(I32))
+
+        def store_scales(cols):
+            rows = out_2.rearrange("h q m -> q h m")
+            for quad in range(4):
+                queue = nc.sync if quad % 2 == 0 or cols.start == 0 else nc.scalar
+                queue.dma_start(
+                    out=rows[4 * quad : 4 * quad + 4, :, cols].bitcast(I32),
+                    in_=out_scales[32 * quad : 32 * quad + 4, :, cols].bitcast(I32),
+                )
+
+        z_pack(0, 0)
+        w_exp(0, 0)
+        z_quant(0, 0)
+        z_pack(0, 1)
+        w_exp(0, 1)
+        w_sub(0, 0)
+        z_quant(0, 1)
+        w_quant(0, 0)
+        for t in range(PACK - Y0_ON_VECTOR):
+            y0_slot(0, t, nc.scalar.copy)
+        w_sub(0, 1)
+        for t in range(PACK - Y0_ON_VECTOR, PACK):
+            y0_slot(0, t, nc.vector.tensor_copy)
+        mu_turn()
+        w_exp(1, 0)
+        w_quant(0, 1)
+        y0_quant(0)
+        z_pack(1, 0)
+        for t in range(PACK):
+            y0_slot(1, t, nc.scalar.copy)
+        w_sub(1, 0)
+        z_quant(1, 0)
+        y1_turn(0)
+        fit_matmul(0)
+        y1_copy(0)
+        w_exp(1, 1)
+        y0_quant(1)
+        w_quant(1, 0)
+        y1_turn(1)
+        fit_matmul(1)
+        y1_copy(1)
+        y1_turn(2)
+        z_pack(1, 1)
+
+        def when(stage, n, *args):
+            if 0 <= n < UNITS:
+                stage(n, *args)
+
+        per_chunk = PASSES * CHUNK // P
+        w_at = {c * per_chunk - W_AHEAD + W_STRIDE * g: (c, g) for c in range(2, CHUNKS) for g in range(PASSES)}
+        w_made = {n + 1: piece for n, piece in w_at.items()}
+        w_made[0] = (1, 1)
+
+        for n in range(UNITS + LAG + 5):
+            u = n - LAG
+            when(dual_step, u)
+            when(residual, n)
+            when(out_exp, u - 1)
+            when(grad_matmul, u + 1)
+            when(residual_turn, n)
+            when(y1_copy, n + 2)
+            when(y1_turn, n + 3)
+            when(weigh, n - 1)
+            if u - 3 < ROUND_ON_VECTOR_FROM:
+                when(out_round, u - 3, nc.scalar.copy)
+            if n in w_made:
+                w_sub(*w_made[n])
+            when(out_sub, u - 2)
+            if n == 0:
+                z_quant(1, 1)
+            if n % 2 == 0 and 0 < n <= UNITS:
+                rl_quant(n // 2 - 1)
+            if n in w_made:
+                w_quant(*w_made[n])
+            if u - 3 >= ROUND_ON_VECTOR_FROM:
+                when(out_round, u - 3, nc.vector.tensor_copy)
+            when(out_quant, u - 4)
+            if u - 4 == EARLY_BLOCKS * PASSES - 1:
+                store_scales(slice(0, EARLY_BLOCKS * P))
+            when(fit_matmul, n + 2)
+            if n in w_at:
+                w_exp(*w_at[n])
+        store_scales(slice(EARLY_BLOCKS * P, N))

@@ -26,14 +26,19 @@ W_FACTOR = 0.05 / 2
 STEP = -0.3 / math.sqrt(N)
 LN_HALF = math.log(0.5)
 LN_FLOOR = 2.0 ** -64
-LAG = 4
-ROUND_ON_VECTOR_FROM = 12
 RL_BUFS = 3
 UNITS = BLOCKS * PASSES
-W_AHEAD = 7
-Y0_ON_VECTOR = 2
-EARLY_BLOCKS = 5
+EARLY_BLOCKS = 4
+HANDOVER = 5
+THETA_WIDTHS = (512, 512)
+Y1_WIDTHS = (256, 256, 512)
+LAG = 5
+SUB_ON_VECTOR_FROM = 10
+ROUND_ON_VECTOR_FROM = 11
+W_FIRST = 0
+YV = 2
 W_STRIDE = 2
+W_DELAY = 2
 
 
 def tile_instrumentedsyntheticcontrolhypentropyst_x1_kernel(
@@ -62,47 +67,58 @@ def tile_instrumentedsyntheticcontrolhypentropyst_x1_kernel(
         lam_sb = kept("lam_sb", [P, PASSES, PACK], BF16)
         mu_rows = kept("mu_rows", [P, P], BF16)
         y0_sb = [[kept("y0_%d_%d" % (g, t), [P, N], BF16) for t in range(PACK)] for g in range(PASSES)]
-        theta_sb = [[kept("theta_%d_%d" % (c, g), [P, PACK, CHUNK], BF16) for g in range(PASSES)] for c in range(CHUNKS)]
-        y1_sb = [[kept("y1_%d_%d" % (c, g), [P, PACK, CHUNK], BF16) for g in range(PASSES)] for c in range(CHUNKS)]
-        z_sb = [[kept("z_%d_%d" % (h, g), [P, PACK, PASS], BF16) for g in range(PASSES)] for h in range(PASSES)]
+
+        def column_tiles(name, widths):
+            starts = [sum(widths[:c]) for c in range(len(widths))]
+            return [
+                (start, [kept("%s_%d_%d" % (name, start, g), [P, PACK, width], BF16) for g in range(PASSES)])
+                for start, width in zip(starts, widths)
+            ]
+
+        theta_sb = column_tiles("theta", THETA_WIDTHS)
+        y1_sb = column_tiles("y1", Y1_WIDTHS)
+        z_sb = column_tiles("z", (PASS, PASS))
         ident_f32 = kept("ident_f32", [P, P], F32)
         ident_bf16 = kept("ident_bf16", [P, P], BF16)
 
-        def load_columns(tiles, x, c):
-            for g in range(PASSES):
-                width = tiles[c][g].shape[2]
-                nc.sync.dma_start(out=tiles[c][g][:], in_=slot_rows(x, g)[:, :, c * width : (c + 1) * width])
-
-        def load_y0(g):
-            for t in range(PACK):
-                nc.sync.dma_start(out=y0_sb[g][t][:], in_=slot_rows(y0, g)[:, t, :])
+        def load_y0(g, t):
+            nc.sync.dma_start(out=y0_sb[g][t][:], in_=slot_rows(y0, g)[:, t, :])
 
         make_identity(nc, ident_f32[:])
         nc.gpsimd.memset(mu_rows[:], 0.0)
         make_identity(nc, ident_bf16[:])
 
         def load_piece(tiles, x, c, g):
-            width = tiles[c][g].shape[2]
-            nc.sync.dma_start(out=tiles[c][g][:], in_=slot_rows(x, g)[:, :, c * width : (c + 1) * width])
+            start, pieces = tiles[c]
+            nc.sync.dma_start(out=pieces[g][:], in_=slot_rows(x, g)[:, :, start : start + pieces[g].shape[2]])
+
+        def columns(tiles, g, first, width):
+            start, pieces = [entry for entry in tiles if entry[0] <= first][-1]
+            return pieces[g][:, :, first - start : first - start + width]
 
         nc.sync.dma_start(out=v_sb[:], in_=v.rearrange("(g p t) -> p g t", g=PASSES, t=PACK))
-        for g in range(PASSES):
-            load_piece(z_sb, z, 0, g)
-            load_piece(theta_sb, theta, 0, g)
-        load_y0(0)
+        load_piece(z_sb, z, 0, 0)
+        load_piece(theta_sb, theta, 0, 0)
+        load_piece(z_sb, z, 0, 1)
+        load_y0(0, 0)
+        load_y0(0, 1)
+        load_piece(theta_sb, theta, 0, 1)
+        load_y0(0, 2)
+        load_y0(0, 3)
         nc.sync.dma_start(out=mu_rows[0:BLOCKS, :], in_=mu.rearrange("(b m) -> b m", m=P))
-        load_piece(theta_sb, theta, 1, 0)
         load_piece(z_sb, z, 1, 0)
-        load_y0(1)
+        for t in range(PACK):
+            load_y0(1, t)
         load_piece(y1_sb, y1, 0, 0)
-        nc.sync.dma_start(out=lam_sb[:], in_=lam.rearrange("(g p t) -> p g t", g=PASSES, t=PACK))
-        load_piece(theta_sb, theta, 1, 1)
-        load_piece(z_sb, z, 1, 1)
         load_piece(y1_sb, y1, 0, 1)
-        load_columns(y1_sb, y1, 1)
-        for c in range(2, CHUNKS):
-            load_columns(theta_sb, theta, c)
-            load_columns(y1_sb, y1, c)
+        nc.sync.dma_start(out=lam_sb[:], in_=lam.rearrange("(g p t) -> p g t", g=PASSES, t=PACK))
+        load_piece(z_sb, z, 1, 1)
+        load_piece(theta_sb, theta, 1, 0)
+        load_piece(y1_sb, y1, 1, 0)
+        load_piece(y1_sb, y1, 1, 1)
+        load_piece(theta_sb, theta, 1, 1)
+        load_piece(y1_sb, y1, 2, 0)
+        load_piece(y1_sb, y1, 2, 1)
 
         slots = PASSES * PACK
         v_flat = v_sb[:].rearrange("p g t -> p (g t)")
@@ -146,13 +162,13 @@ def tile_instrumentedsyntheticcontrolhypentropyst_x1_kernel(
         w_state = {}
 
         def w_exp(c, g):
-            up = passing("w_up", [P, PACK, CHUNK], F32)
-            down = passing("w_down", [P, PACK, CHUNK], F32)
+            up = passing("w_up", [P, PACK, CHUNK], F32, bufs=3)
+            down = passing("w_down", [P, PACK, CHUNK], F32, bufs=3)
             for t in range(PACK):
                 s = g * PACK + t
                 for dst, sign in ((up, v_sign), (down, v_sign_neg)):
                     nc.scalar.activation(
-                        out=dst[:, t, :], in_=theta_sb[c][g][:, t, :], func=ACT.Exp,
+                        out=dst[:, t, :], in_=columns(theta_sb, g, c * CHUNK, CHUNK)[:, t, :], func=ACT.Exp,
                         scale=sign[:, s : s + 1], bias=v_log[:, s : s + 1],
                     )
             w_state[c, g] = (up, down)
@@ -179,11 +195,11 @@ def tile_instrumentedsyntheticcontrolhypentropyst_x1_kernel(
         z_scales = [[kept("z_scales%d_%d" % (h, g), [P, PASS], U8) for g in range(PASSES)] for h in range(PASSES)]
         z_state = {}
 
-        def z_pack(h, g):
+        def z_pack(h, g, copy=nc.vector.tensor_copy):
             packed = passing("z_packed", [P, PACK, P, PACK], BF16)
-            nc.vector.tensor_copy(
+            copy(
                 out=packed[:].rearrange("p s (q i) t -> p q s i t", i=2),
-                in_=z_sb[h][g][:].rearrange("p t (q i s) -> p q s i t", i=2, s=PACK),
+                in_=columns(z_sb, g, h * PASS, PASS).rearrange("p t (q i s) -> p q s i t", i=2, s=PACK),
             )
             z_state[h, g] = packed
 
@@ -208,17 +224,17 @@ def tile_instrumentedsyntheticcontrolhypentropyst_x1_kernel(
             c, half = divmod(b, CHUNK // P)
             return b, g, c, slice(half * P, (half + 1) * P)
 
-        def y1_turn(n):
-            b, g, c, cols = place(n)
-            turned = bank("y1_bank%d" % g, [P, PACK, P], BF16)
-            for t in range(PACK):
-                nc.tensor.transpose(turned[:, t, :], y1_sb[c][g][:, t, cols], ident_bf16[:])
-            y1_t[n] = turned
+        def y1_turn(b):
+            turned = bank("y1_bank%d" % (b % 2), [P, PASSES, PACK, P], BF16)
+            for g in range(PASSES):
+                for t in range(PACK):
+                    nc.tensor.transpose(turned[:, g, t, :], columns(y1_sb, g, b * P, P)[:, t, :], ident_bf16[:])
+            y1_t[b] = turned
 
-        def y1_copy(n):
-            dst = passing("y1_t", [P, PASS], BF16, bufs=3)
-            nc.scalar.copy(out=dst[:], in_=y1_t[n][:].rearrange("p t r -> p (t r)"))
-            y1_t[n] = dst
+        def y1_copy(b):
+            dst = passing("y1_t", [P, PASSES, PASS], BF16)
+            nc.scalar.copy(out=dst[:].rearrange("p g c -> p (g c)"), in_=y1_t[b][:].rearrange("p g t r -> p (g t r)"))
+            y1_t[b] = dst
 
         def fit_matmul(n):
             b, g, c, cols = place(n)
@@ -239,7 +255,7 @@ def tile_instrumentedsyntheticcontrolhypentropyst_x1_kernel(
             b, g, c, cols = place(n)
             r = passing("resid", [P, PASS], F32)
             nc.vector.scalar_tensor_tensor(
-                out=r[:], in0=fit[n][:], scalar=mu_col[:, b : b + 1], in1=y1_t[n][:],
+                out=r[:], in0=fit[n][:], scalar=mu_col[:, b : b + 1], in1=y1_t[b][:, g, :],
                 op0=ALU.add, op1=ALU.subtract,
             )
             resid[n] = r
@@ -252,22 +268,26 @@ def tile_instrumentedsyntheticcontrolhypentropyst_x1_kernel(
 
         def weigh(n):
             b, g, c, cols = place(n)
-            if g == 0:
-                rl[b] = passing("rl_packed", [P, PASSES, P, PACK], BF16)
+            rl[n] = keep.tile([P, P, PACK], BF16, name="rl_packed", tag="handover%d" % (n % HANDOVER), align_bytes=64)
             nc.vector.tensor_tensor(
-                out=rl[b][:, g, :, :],
+                out=rl[n][:],
                 in0=back[n][:].rearrange("p t m -> p m t"),
                 in1=lam_sb[:, g, :].unsqueeze(1).to_broadcast([P, P, PACK]),
                 op=ALU.mult,
             )
 
-        def rl_quant(b):
-            codes = passing("rl_codes", [P, PASSES * P], U32, bufs=RL_BUFS)
-            scales = passing("rl_scales", [P, PASSES * P], U8, bufs=RL_BUFS)
+        def rl_quant(n):
+            b, g, c, cols = place(n)
+            if g == 0:
+                codes = passing("rl_codes", [P, PASSES * P], U32, bufs=RL_BUFS)
+                scales = passing("rl_scales", [P, PASSES * P], U8, bufs=RL_BUFS)
+                rl_q[b] = (codes, scales)
+            codes, scales = rl_q[b]
             nc.vector.quantize_mx(
-                out=codes[:].bitcast(FP8X4), scales=scales[:], in_=rl[b][:].rearrange("p g m t -> p (g m t)")
+                out=codes[:, g * P : (g + 1) * P].bitcast(FP8X4),
+                scales=scales[:, g * P : (g + 1) * P],
+                in_=rl[n][:].rearrange("p m t -> p (m t)"),
             )
-            rl_q[b] = (codes, scales)
 
         grad, stepped, exps, result, rounded, out_codes = {}, {}, {}, {}, {}, {}
         out_scales = kept("out_scales", [P, PASSES, N], U8)
@@ -293,7 +313,7 @@ def tile_instrumentedsyntheticcontrolhypentropyst_x1_kernel(
             b, h, c, cols = place(n)
             stepped[n] = passing("theta2", [P, PACK, P], F32, bufs=3)
             nc.vector.scalar_tensor_tensor(
-                out=stepped[n][:], in0=grad[n][:], scalar=STEP, in1=theta_sb[c][h][:, :, cols],
+                out=stepped[n][:], in0=grad[n][:], scalar=STEP, in1=columns(theta_sb, h, b * P, P),
                 op0=ALU.mult, op1=ALU.add,
             )
 
@@ -304,11 +324,11 @@ def tile_instrumentedsyntheticcontrolhypentropyst_x1_kernel(
             nc.scalar.activation(out=down[:], in_=stepped[n][:], func=ACT.Exp, scale=-1.0, bias=LN_HALF)
             exps[n] = (up, down)
 
-        def out_sub(n):
+        def out_sub(n, engine):
             b, h, c, cols = place(n)
             up, down = exps[n]
-            res = passing("result", [P, PACK, P], F32, bufs=5)
-            nc.vector.tensor_tensor(out=res[:], in0=up[:], in1=down[:], op=ALU.subtract)
+            res = keep.tile([P, PACK, P], F32, name="result", tag="handover%d" % ((n + LAG - 1) % HANDOVER), align_bytes=64)
+            engine.tensor_tensor(out=res[:], in0=up[:], in1=down[:], op=ALU.subtract)
             nc.sync.dma_start(out=slot_rows(out_0, h)[:, :, b * P : (b + 1) * P], in_=res[:])
             result[n] = res
 
@@ -346,45 +366,42 @@ def tile_instrumentedsyntheticcontrolhypentropyst_x1_kernel(
         w_exp(0, 0)
         z_quant(0, 0)
         z_pack(0, 1)
-        w_exp(0, 1)
+        w_exp(1, 0)
         w_sub(0, 0)
         z_quant(0, 1)
+        y0_slot(0, 0, nc.vector.tensor_copy)
         w_quant(0, 0)
-        for t in range(PACK - Y0_ON_VECTOR):
-            y0_slot(0, t, nc.scalar.copy)
+        y0_slot(0, 1, nc.vector.tensor_copy if YV > 1 else nc.scalar.copy)
+        w_exp(0, 1)
+        w_sub(1, 0)
+        y0_slot(0, 2, nc.vector.tensor_copy if YV > 2 else nc.scalar.copy)
+        y0_slot(0, 3, nc.vector.tensor_copy if YV > 3 else nc.scalar.copy)
+        w_exp(1, 1)
         w_sub(0, 1)
-        for t in range(PACK - Y0_ON_VECTOR, PACK):
-            y0_slot(0, t, nc.vector.tensor_copy)
-        mu_turn()
-        w_exp(1, 0)
-        w_quant(0, 1)
+        w_quant(1, 0)
         y0_quant(0)
-        z_pack(1, 0)
+        w_quant(0, 1)
+        mu_turn()
         for t in range(PACK):
             y0_slot(1, t, nc.scalar.copy)
-        w_sub(1, 0)
-        z_quant(1, 0)
         y1_turn(0)
         fit_matmul(0)
+        z_pack(1, 0)
+        w_sub(1, 1)
+        z_quant(1, 0)
+        w_quant(1, 1)
         y1_copy(0)
-        w_exp(1, 1)
         y0_quant(1)
-        w_quant(1, 0)
-        y1_turn(1)
         fit_matmul(1)
-        y1_copy(1)
-        y1_turn(2)
-        z_pack(1, 1)
 
         def when(stage, n, *args):
             if 0 <= n < UNITS:
                 stage(n, *args)
 
-        per_chunk = PASSES * CHUNK // P
-        w_at = {c * per_chunk - W_AHEAD + W_STRIDE * g: (c, g) for c in range(2, CHUNKS) for g in range(PASSES)}
-        w_made = {n + 1: piece for n, piece in w_at.items()}
-        w_made[0] = (1, 1)
+        def round_on_vector(u):
+            return u >= ROUND_ON_VECTOR_FROM and u % 2 == 1
 
+        w_at = {W_FIRST + W_STRIDE * i: (2 + i // PASSES, i % PASSES) for i in range(2 * PASSES)}
         for n in range(UNITS + LAG + 5):
             u = n - LAG
             when(dual_step, u)
@@ -392,23 +409,29 @@ def tile_instrumentedsyntheticcontrolhypentropyst_x1_kernel(
             when(out_exp, u - 1)
             when(grad_matmul, u + 1)
             when(residual_turn, n)
-            when(y1_copy, n + 2)
-            when(y1_turn, n + 3)
+            if n % 2 == 1 and n // 2 + 1 < BLOCKS:
+                y1_copy(n // 2 + 1)
+            if n % 2 == 0 and n // 2 + 1 < BLOCKS:
+                y1_turn(n // 2 + 1)
             when(weigh, n - 1)
-            if u - 3 < ROUND_ON_VECTOR_FROM:
+            if not round_on_vector(u - 3):
                 when(out_round, u - 3, nc.scalar.copy)
-            if n in w_made:
-                w_sub(*w_made[n])
-            when(out_sub, u - 2)
+            if u - 2 < SUB_ON_VECTOR_FROM:
+                when(out_sub, u - 2, nc.gpsimd)
             if n == 0:
-                z_quant(1, 1)
-            if n % 2 == 0 and 0 < n <= UNITS:
-                rl_quant(n // 2 - 1)
-            if n in w_made:
-                w_quant(*w_made[n])
-            if u - 3 >= ROUND_ON_VECTOR_FROM:
+                z_pack(1, 1)
+            if n - W_DELAY in w_at:
+                w_sub(*w_at[n - W_DELAY])
+            if u - 2 >= SUB_ON_VECTOR_FROM:
+                when(out_sub, u - 2, nc.vector)
+            if round_on_vector(u - 3):
                 when(out_round, u - 3, nc.vector.tensor_copy)
+            if n == 1:
+                z_quant(1, 1)
+            if n - W_DELAY - 1 in w_at:
+                w_quant(*w_at[n - W_DELAY - 1])
             when(out_quant, u - 4)
+            when(rl_quant, n - 2)
             if u - 4 == EARLY_BLOCKS * PASSES - 1:
                 store_scales(slice(0, EARLY_BLOCKS * P))
             when(fit_matmul, n + 2)

@@ -37,7 +37,7 @@ SUB_ON_VECTOR_FROM = 10
 ROUND_ON_VECTOR_FROM = 11
 W_FIRST = 0
 YV = 2
-W_STRIDE = 2
+W_STEPS = (0, 2, 4, 6)
 W_DELAY = 2
 
 
@@ -232,7 +232,7 @@ def tile_instrumentedsyntheticcontrolhypentropyst_x1_kernel(
             y1_t[b] = turned
 
         def y1_copy(b):
-            dst = passing("y1_t", [P, PASSES, PASS], BF16)
+            dst = passing("y1_t", [P, PASSES, PASS], BF16, bufs=5)
             nc.scalar.copy(out=dst[:].rearrange("p g c -> p (g c)"), in_=y1_t[b][:].rearrange("p g t r -> p (g t r)"))
             y1_t[b] = dst
 
@@ -401,7 +401,7 @@ def tile_instrumentedsyntheticcontrolhypentropyst_x1_kernel(
         def round_on_vector(u):
             return u >= ROUND_ON_VECTOR_FROM and u % 2 == 1
 
-        w_at = {W_FIRST + W_STRIDE * i: (2 + i // PASSES, i % PASSES) for i in range(2 * PASSES)}
+        w_at = {n: (2 + i // PASSES, i % PASSES) for i, n in enumerate(W_STEPS)}
         for n in range(UNITS + LAG + 5):
             u = n - LAG
             when(dual_step, u)
@@ -409,10 +409,10 @@ def tile_instrumentedsyntheticcontrolhypentropyst_x1_kernel(
             when(out_exp, u - 1)
             when(grad_matmul, u + 1)
             when(residual_turn, n)
-            if n % 2 == 1 and n // 2 + 1 < BLOCKS:
-                y1_copy(n // 2 + 1)
-            if n % 2 == 0 and n // 2 + 1 < BLOCKS:
-                y1_turn(n // 2 + 1)
+            if 0 < n < BLOCKS:
+                y1_copy(n)
+            if n + 1 < BLOCKS:
+                y1_turn(n + 1)
             when(weigh, n - 1)
             if not round_on_vector(u - 3):
                 when(out_round, u - 3, nc.scalar.copy)
@@ -430,8 +430,8 @@ def tile_instrumentedsyntheticcontrolhypentropyst_x1_kernel(
                 z_quant(1, 1)
             if n - W_DELAY - 1 in w_at:
                 w_quant(*w_at[n - W_DELAY - 1])
-            when(out_quant, u - 4)
             when(rl_quant, n - 2)
+            when(out_quant, u - 4)
             if u - 4 == EARLY_BLOCKS * PASSES - 1:
                 store_scales(slice(0, EARLY_BLOCKS * P))
             when(fit_matmul, n + 2)

import math
from contextlib import ExitStack

import concourse.mybir as mybir
from concourse.masks import make_identity

F32 = mybir.dt.float32
BF16 = mybir.dt.bfloat16
U32 = mybir.dt.uint32
I32 = mybir.dt.int32
U8 = mybir.dt.uint8
FP8X4 = mybir.dt.float8_e4m3fn_x4
ALU = mybir.AluOpType
ACT = mybir.ActivationFunctionType

N = 1024
FLOPS = 2 * 2 * N * N * N
P = 128
PACK = 4
PASS = P * PACK
PASSES = N // PASS
BLOCKS = N // P
CHUNK = 256
CHUNKS = N // CHUNK
W_FACTOR = 0.05 / 2
STEP = -0.3 / math.sqrt(N)
LN_HALF = math.log(0.5)
LN_FLOOR = 2.0 ** -64
RL_BUFS = 3
UNITS = BLOCKS * PASSES
EARLY_BLOCKS = 4
HANDOVER = 5
THETA_WIDTHS = (512, 512)
Y1_WIDTHS = (256, 256, 512)
LAG = 5
SUB_ON_VECTOR_FROM = 10
ROUND_ON_VECTOR_FROM = 11
W_FIRST = 0
YV = 2
W_STEPS = (0, 2, 4, 6)
W_DELAY = 2


def tile_instrumentedsyntheticcontrolhypentropyst_x1_kernel(
    tc, y0, y1, z, theta, v, lam, mu, out_0, out_1, out_2
):
    nc = tc.nc
    with ExitStack() as ctx:
        keep = ctx.enter_context(tc.tile_pool(name="keep", bufs=1))
        work = ctx.enter_context(tc.tile_pool(name="work", bufs=2))
        psum = ctx.enter_context(tc.psum_pool(name="psum", bufs=1))
        ctx.enter_context(tc.manual_schedule())

        def kept(name, shape, dtype):
            return keep.tile(shape, dtype, name=name, align_bytes=64)

        def passing(name, shape, dtype, bufs=2):
            return work.tile(shape, dtype, name=name, align_bytes=64, bufs=bufs)

        def bank(tag, shape, dtype):
            return psum.tile(shape, dtype, name=tag)

        def slot_rows(x, g):
            return x[g * PASS : (g + 1) * PASS, :].rearrange("(p t) c -> p t c", t=PACK)

        v_sb = kept("v_sb", [P, PASSES, PACK], BF16)
        lam_sb = kept("lam_sb", [P, PASSES, PACK], BF16)
        mu_rows = kept("mu_rows", [P, P], BF16)
        y0_sb = [[kept("y0_%d_%d" % (g, t), [P, N], BF16) for t in range(PACK)] for g in range(PASSES)]

        def column_tiles(name, widths):
            starts = [sum(widths[:c]) for c in range(len(widths))]
            return [
                (start, [kept("%s_%d_%d" % (name, start, g), [P, PACK, width], BF16) for g in range(PASSES)])
                for start, width in zip(starts, widths)
            ]

        theta_sb = column_tiles("theta", THETA_WIDTHS)
        y1_sb = column_tiles("y1", Y1_WIDTHS)
        z_sb = column_tiles("z", (PASS, PASS))
        ident_f32 = kept("ident_f32", [P, P], F32)
        ident_bf16 = kept("ident_bf16", [P, P], BF16)

        def load_y0(g, t):
            nc.sync.dma_start(out=y0_sb[g][t][:], in_=slot_rows(y0, g)[:, t, :])

        make_identity(nc, ident_f32[:])
        nc.gpsimd.memset(mu_rows[:], 0.0)
        make_identity(nc, ident_bf16[:])

        def load_piece(tiles, x, c, g):
            start, pieces = tiles[c]
            nc.sync.dma_start(out=pieces[g][:], in_=slot_rows(x, g)[:, :, start : start + pieces[g].shape[2]])

        def columns(tiles, g, first, width):
            start, pieces = [entry for entry in tiles if entry[0] <= first][-1]
            return pieces[g][:, :, first - start : first - start + width]

        nc.sync.dma_start(out=v_sb[:], in_=v.rearrange("(g p t) -> p g t", g=PASSES, t=PACK))
        load_piece(z_sb, z, 0, 0)
        load_piece(theta_sb, theta, 0, 0)
        load_piece(z_sb, z, 0, 1)
        load_y0(0, 0)
        load_y0(0, 1)
        load_piece(theta_sb, theta, 0, 1)
        load_y0(0, 2)
        load_y0(0, 3)
        nc.sync.dma_start(out=mu_rows[0:BLOCKS, :], in_=mu.rearrange("(b m) -> b m", m=P))
        load_piece(z_sb, z, 1, 0)
        for t in range(PACK):
            load_y0(1, t)
        load_piece(y1_sb, y1, 0, 0)
        load_piece(y1_sb, y1, 0, 1)
        nc.sync.dma_start(out=lam_sb[:], in_=lam.rearrange("(g p t) -> p g t", g=PASSES, t=PACK))
        load_piece(z_sb, z, 1, 1)
        load_piece(theta_sb, theta, 1, 0)
        load_piece(y1_sb, y1, 1, 0)
        load_piece(y1_sb, y1, 1, 1)
        load_piece(theta_sb, theta, 1, 1)
        load_piece(y1_sb, y1, 2, 0)
        load_piece(y1_sb, y1, 2, 1)

        slots = PASSES * PACK
        v_flat = v_sb[:].rearrange("p g t -> p (g t)")
        v_abs = kept("v_abs", [P, slots], F32)
        v_pos = kept("v_pos", [P, slots], F32)
        v_neg = kept("v_neg", [P, slots], F32)
        v_sign = kept("v_sign", [P, slots], F32)
        v_sign_neg = kept("v_sign_neg", [P, slots], F32)
        v_log = kept("v_log", [P, slots], F32)
        nc.vector.scalar_tensor_tensor(out=v_abs[:], in0=v_flat, scalar=-1.0, in1=v_flat, op0=ALU.mult, op1=ALU.max)
        nc.vector.tensor_scalar(out=v_pos[:], in0=v_flat, scalar1=0.0, scalar2=None, op0=ALU.is_gt)
        nc.vector.tensor_scalar(out=v_neg[:], in0=v_flat, scalar1=0.0, scalar2=None, op0=ALU.is_lt)
        nc.scalar.activation(out=v_log[:], in_=v_abs[:], func=ACT.Ln, scale=W_FACTOR, bias=LN_FLOOR)
        nc.vector.tensor_tensor(out=v_sign[:], in0=v_pos[:], in1=v_neg[:], op=ALU.subtract)
        nc.vector.tensor_tensor(out=v_sign_neg[:], in0=v_neg[:], in1=v_pos[:], op=ALU.subtract)

        y0_words = [kept("y0_words%d" % g, [P, PASSES, PASS, 2], F32) for g in range(PASSES)]
        y0_codes = [kept("y0_codes%d" % g, [P, N], U32) for g in range(PASSES)]
        y0_scales = [kept("y0_scales%d" % g, [P, N], U8) for g in range(PASSES)]
        y0_banks = ["turn0", "turn1", "grad0", "grad1"]

        def y0_slot(g, t, copy):
            turned = bank(y0_banks[t], [P, PASSES, 2, P], F32)
            words = y0_sb[g][t][:].bitcast(F32)
            for k in range(PASSES):
                for u in range(2):
                    nc.tensor.transpose(turned[:, k, u, :], words[:, 2 * P * k + u : 2 * P * (k + 1) : 2], ident_f32[:])
            copy(
                out=y0_words[g][:, :, t * P : (t + 1) * P, :], in_=turned[:].rearrange("p k u r -> p k r u")
            )

        def y0_quant(g):
            nc.vector.quantize_mx(
                out=y0_codes[g][:].bitcast(FP8X4),
                scales=y0_scales[g][:],
                in_=y0_words[g][:].rearrange("p k c u -> p (k c u)").bitcast(BF16),
            )

        w_codes = [kept("w_codes%d" % c, [P, PASSES, CHUNK], U32) for c in range(CHUNKS)]
        w_scales = [kept("w_scales%d" % c, [P, PASSES, CHUNK], U8) for c in range(CHUNKS)]
        w_state = {}

        def w_exp(c, g):
            up = passing("w_up", [P, PACK, CHUNK], F32, bufs=3)
            down = passing("w_down", [P, PACK, CHUNK], F32, bufs=3)
            for t in range(PACK):
                s = g * PACK + t
                for dst, sign in ((up, v_sign), (down, v_sign_neg)):
                    nc.scalar.activation(
                        out=dst[:, t, :], in_=columns(theta_sb, g, c * CHUNK, CHUNK)[:, t, :], func=ACT.Exp,
                        scale=sign[:, s : s + 1], bias=v_log[:, s : s + 1],
                    )
            w_state[c, g] = (up, down)

        def w_sub(c, g):
            up, down = w_state[c, g]
            packed = passing("w_packed", [P, CHUNK, PACK], BF16)
            nc.vector.tensor_tensor(
                out=packed[:].rearrange("p (m i) t -> p m t i", i=2),
                in0=up[:].rearrange("p t (m i) -> p m t i", i=2),
                in1=down[:].rearrange("p t (m i) -> p m t i", i=2),
                op=ALU.subtract,
            )
            w_state[c, g] = packed

        def w_quant(c, g):
            nc.vector.quantize_mx(
                out=w_codes[c][:, g, :].bitcast(FP8X4),
                scales=w_scales[c][:, g, :],
                in_=w_state[c, g][:].rearrange("p m t -> p (m t)"),
            )

        z_codes = [[kept("z_codes%d_%d" % (h, g), [P, PASS], U32) for g in range(PASSES)] for h in range(PASSES)]
        z_scales = [[kept("z_scales%d_%d" % (h, g), [P, PASS], U8) for g in range(PASSES)] for h in range(PASSES)]
        z_state = {}

        def z_pack(h, g, copy=nc.vector.tensor_copy):
            packed = passing("z_packed", [P, PACK, P, PACK], BF16)
            copy(
                out=packed[:].rearrange("p s (q i) t -> p q s i t", i=2),
                in_=columns(z_sb, g, h * PASS, PASS).rearrange("p t (q i s) -> p q s i t", i=2, s=PACK),
            )
            z_state[h, g] = packed

        def z_quant(h, g):
            nc.vector.quantize_mx(
                out=z_codes[h][g][:].bitcast(FP8X4),
                scales=z_scales[h][g][:],
                in_=z_state[h, g][:].rearrange("p s q t -> p (s q t)"),
            )

        mu_col = kept("mu_col", [P, BLOCKS], F32)

        def mu_turn():
            turned = bank("y1_bank1", [P, P], BF16)
            nc.tensor.transpose(turned[:], mu_rows[:], ident_bf16[:])
            nc.scalar.copy(out=mu_col[:], in_=turned[:, 0:BLOCKS])

        y1_t, fit, resid, back, rl, rl_q = {}, {}, {}, {}, {}, {}

        def place(n):
            b, g = divmod(n, PASSES)
            c, half = divmod(b, CHUNK // P)
            return b, g, c, slice(half * P, (half + 1) * P)

        def y1_turn(b):
            turned = bank("y1_bank%d" % (b % 2), [P, PASSES, PACK, P], BF16)
            for g in range(PASSES):
                for t in range(PACK):
                    nc.tensor.transpose(turned[:, g, t, :], columns(y1_sb, g, b * P, P)[:, t, :], ident_bf16[:])
            y1_t[b] = turned

        def y1_copy(b):
            dst = passing("y1_t", [P, PASSES, PASS], BF16, bufs=5)
            nc.scalar.copy(out=dst[:].rearrange("p g c -> p (g c)"), in_=y1_t[b][:].rearrange("p g t r -> p (g t r)"))
            y1_t[b] = dst

        def fit_matmul(n):
            b, g, c, cols = place(n)
            acc = bank("fit%d" % g, [P, PASS], F32)
            for k in range(PASSES):
                nc.tensor.matmul_mx(
                    out=acc[:],
                    lhsT=w_codes[c][:, k, cols].bitcast(FP8X4),
                    lhsT_scale=w_scales[c][:, k, cols],
                    rhs=y0_codes[g][:, k * PASS : (k + 1) * PASS].bitcast(FP8X4),
                    rhs_scale=y0_scales[g][:, k * PASS : (k + 1) * PASS],
                    start=(k == 0),
                    stop=(k == PASSES - 1),
                )
            fit[n] = acc

        def residual(n):
            b, g, c, cols = place(n)
            r = passing("resid", [P, PASS], F32)
            nc.vector.scalar_tensor_tensor(
                out=r[:], in0=fit[n][:], scalar=mu_col[:, b : b + 1], in1=y1_t[b][:, g, :],
                op0=ALU.add, op1=ALU.subtract,
            )
            resid[n] = r

        def residual_turn(n):
            turned = bank("turn%d" % (n % PASSES), [P, PACK, P], F32)
            for t in range(PACK):
                nc.tensor.transpose(turned[:, t, :], resid[n][:, t * P : (t + 1) * P], ident_f32[:])
            back[n] = turned

        def weigh(n):
            b, g, c, cols = place(n)
            rl[n] = keep.tile([P, P, PACK], BF16, name="rl_packed", tag="handover%d" % (n % HANDOVER), align_bytes=64)
            nc.vector.tensor_tensor(
                out=rl[n][:],
                in0=back[n][:].rearrange("p t m -> p m t"),
                in1=lam_sb[:, g, :].unsqueeze(1).to_broadcast([P, P, PACK]),
                op=ALU.mult,
            )

        def rl_quant(n):
            b, g, c, cols = place(n)
            if g == 0:
                codes = passing("rl_codes", [P, PASSES * P], U32, bufs=RL_BUFS)
                scales = passing("rl_scales", [P, PASSES * P], U8, bufs=RL_BUFS)
                rl_q[b] = (codes, scales)
            codes, scales = rl_q[b]
            nc.vector.quantize_mx(
                out=codes[:, g * P : (g + 1) * P].bitcast(FP8X4),
                scales=scales[:, g * P : (g + 1) * P],
                in_=rl[n][:].rearrange("p m t -> p (m t)"),
            )

        grad, stepped, exps, result, rounded, out_codes = {}, {}, {}, {}, {}, {}
        out_scales = kept("out_scales", [P, PASSES, N], U8)

        def grad_matmul(n):
            b, h, c, cols = place(n)
            codes, scales = rl_q[b]
            acc = bank("grad%d" % h, [P, PACK, P], F32)
            for s in range(PACK):
                for g in range(PASSES):
                    nc.tensor.matmul_mx(
                        out=acc[:, s, :],
                        lhsT=z_codes[h][g][:, s * P : (s + 1) * P].bitcast(FP8X4),
                        lhsT_scale=z_scales[h][g][:, s * P : (s + 1) * P],
                        rhs=codes[:, g * P : (g + 1) * P].bitcast(FP8X4),
                        rhs_scale=scales[:, g * P : (g + 1) * P],
                        start=(g == 0),
                        stop=(g == PASSES - 1),
                    )
            grad[n] = acc

        def dual_step(n):
            b, h, c, cols = place(n)
            stepped[n] = passing("theta2", [P, PACK, P], F32, bufs=3)
            nc.vector.scalar_tensor_tensor(
                out=stepped[n][:], in0=grad[n][:], scalar=STEP, in1=columns(theta_sb, h, b * P, P),
                op0=ALU.mult, op1=ALU.add,
            )

        def out_exp(n):
            up = passing("out_up", [P, PACK, P], F32, bufs=3)
            down = passing("out_down", [P, PACK, P], F32, bufs=3)
            nc.scalar.activation(out=up[:], in_=stepped[n][:], func=ACT.Exp, scale=1.0, bias=LN_HALF)
            nc.scalar.activation(out=down[:], in_=stepped[n][:], func=ACT.Exp, scale=-1.0, bias=LN_HALF)
            exps[n] = (up, down)

        def out_sub(n, engine):
            b, h, c, cols = place(n)
            up, down = exps[n]
            res = keep.tile([P, PACK, P], F32, name="result", tag="handover%d" % ((n + LAG - 1) % HANDOVER), align_bytes=64)
            engine.tensor_tensor(out=res[:], in0=up[:], in1=down[:], op=ALU.subtract)
            nc.sync.dma_start(out=slot_rows(out_0, h)[:, :, b * P : (b + 1) * P], in_=res[:])
            result[n] = res

        def out_round(n, copy):
            packed = passing("out_packed", [P, P, PACK], BF16, bufs=3)
            copy(
                out=packed[:].rearrange("p (m i) s -> p m s i", i=2),
                in_=result[n][:].rearrange("p s (m i) -> p m s i", i=2),
            )
            rounded[n] = packed

        def out_quant(n):
            b, h, c, cols = place(n)
            if h == 0:
                out_codes[b] = passing("out_codes", [P, PASSES, P], U32, bufs=3)
            nc.vector.quantize_mx(
                out=out_codes[b][:, h, :].bitcast(FP8X4),
                scales=out_scales[:, h, b * P : (b + 1) * P],
                in_=rounded[n][:].rearrange("p m s -> p (m s)"),
            )
            if h == PASSES - 1:
                words = out_1.rearrange("h p m s -> p h (m s)").bitcast(I32)
                nc.sync.dma_start(out=words[:, :, b * P : (b + 1) * P], in_=out_codes[b][:].bitcast(I32))

        def store_scales(cols):
            rows = out_2.rearrange("h q m -> q h m")
            for quad in range(4):
                queue = nc.sync if quad % 2 == 0 or cols.start == 0 else nc.scalar
                queue.dma_start(
                    out=rows[4 * quad : 4 * quad + 4, :, cols].bitcast(I32),
                    in_=out_scales[32 * quad : 32 * quad + 4, :, cols].bitcast(I32),
                )

        z_pack(0, 0)
        w_exp(0, 0)
        z_quant(0, 0)
        z_pack(0, 1)
        w_exp(1, 0)
        w_sub(0, 0)
        z_quant(0, 1)
        y0_slot(0, 0, nc.vector.tensor_copy)
        w_quant(0, 0)
        y0_slot(0, 1, nc.vector.tensor_copy if YV > 1 else nc.scalar.copy)
        w_exp(0, 1)
        w_sub(1, 0)
        y0_slot(0, 2, nc.vector.tensor_copy if YV > 2 else nc.scalar.copy)
        y0_slot(0, 3, nc.vector.tensor_copy if YV > 3 else nc.scalar.copy)
        w_exp(1, 1)
        w_sub(0, 1)
        w_quant(1, 0)
        y0_quant(0)
        w_quant(0, 1)
        mu_turn()
        for t in range(PACK):
            y0_slot(1, t, nc.scalar.copy)
        y1_turn(0)
        fit_matmul(0)
        z_pack(1, 0)
        w_sub(1, 1)
        z_quant(1, 0)
        w_quant(1, 1)
        y1_copy(0)
        y0_quant(1)
        fit_matmul(1)

        def when(stage, n, *args):
            if 0 <= n < UNITS:
                stage(n, *args)

        def round_on_vector(u):
            return u >= ROUND_ON_VECTOR_FROM and u % 2 == 1

        w_at = {n: (2 + i // PASSES, i % PASSES) for i, n in enumerate(W_STEPS)}
        for n in range(UNITS + LAG + 5):
            u = n - LAG
            when(dual_step, u)
            when(residual, n)
            when(out_exp, u - 1)
            when(grad_matmul, u + 1)
            when(residual_turn, n)
            if 0 < n < BLOCKS:
                y1_copy(n)
            if n + 1 < BLOCKS:
                y1_turn(n + 1)
            when(weigh, n - 1)
            if not round_on_vector(u - 3):
                when(out_round, u - 3, nc.scalar.copy)
            if u - 2 < SUB_ON_VECTOR_FROM:
                when(out_sub, u - 2, nc.gpsimd)
            if n == 0:
                z_pack(1, 1)
            if n - W_DELAY in w_at:
                w_sub(*w_at[n - W_DELAY])
            if u - 2 >= SUB_ON_VECTOR_FROM:
                when(out_sub, u - 2, nc.vector)
            if round_on_vector(u - 3):
                when(out_round, u - 3, nc.vector.tensor_copy)
            if n == 1:
                z_quant(1, 1)
            if n - W_DELAY - 1 in w_at:
                w_quant(*w_at[n - W_DELAY - 1])
            when(rl_quant, n - 2)
            when(out_quant, u - 4)
            if u - 4 == EARLY_BLOCKS * PASSES - 1:
                store_scales(slice(0, EARLY_BLOCKS * P))
            when(fit_matmul, n + 2)
            if n in w_at:
                w_exp(*w_at[n])
        store_scales(slice(EARLY_BLOCKS * P, N))
